import numpy as np
import ml_dtypes


def mxq(x, axis, fmt="e4m3"):
    dtype, down = {"e4m3": (ml_dtypes.float8_e4m3fn, 7), "e5m2": (ml_dtypes.float8_e5m2, 14)}[fmt]
    v = np.moveaxis(np.asarray(x, np.float32).astype(ml_dtypes.bfloat16).astype(np.float64), axis, -1)
    blocks = v.reshape(v.shape[:-1] + (-1, 32))
    amax = np.abs(blocks).max(-1, keepdims=True)
    byte = np.maximum(np.where(amax > 0, np.frexp(amax)[1] - 1 + 127, 0) - down, 1)
    scale = np.exp2(byte - 127.0)
    codes = (blocks / scale).astype(np.float32).astype(dtype).astype(np.float64)
    return np.moveaxis((codes * scale).reshape(v.shape), -1, axis)


WIDE = False


def mx_kscale(k):
    if not WIDE:
        return np.ones(k)
    levels = np.array([10, -10, 5, -5, 0])
    if k % 512:
        return np.exp2(np.random.permutation(np.resize(levels, k // 32))).repeat(32)
    a = np.empty((k // 512, 16))
    for p in range(k // 512):
        a[p, :8] = np.random.permutation(np.resize(levels, 8))
        for g in range(8):
            far = levels[np.abs(levels - a[p, g]) >= 10]
            a[p, g + 8] = far[np.random.randint(len(far))]
    return np.exp2(a.ravel()).repeat(32)


def f64(x):
    return np.asarray(x).astype(np.float64)


def striped8(idx):
    return np.concatenate([x.reshape(-1, 16).T for x in idx]).astype(np.uint16)


def runs(offs, k):
    lists = np.stack([offs[16 * r : 16 * r + 16].T.reshape(-1) for r in range(8)]).astype(np.int64)
    return lists[np.arange(k) % 512 // 64]


def pack_weight(w):
    k, n = w.shape
    w = f64(np.asarray(w, np.float32).astype(ml_dtypes.bfloat16)).reshape(k // 32, 32, n)
    amax = np.abs(w).max(1)
    byte = np.clip(np.where(amax > 0, np.frexp(amax)[1] - 1 + 127 - 7, 1), 1, 254)
    scaled = (w * np.exp2(127.0 - byte)[:, None, :]).reshape(k, n).astype(np.float32)
    words = np.ascontiguousarray(scaled.reshape(k // 512, 128, 4, n).transpose(0, 1, 3, 2)).astype(ml_dtypes.float8_e4m3fn).view(np.uint8)
    return words, np.ascontiguousarray(byte.astype(np.uint8).reshape(k // 512, 16, n))


def unpack_weight(words, scales):
    g, p, n, _ = words.shape
    vals = np.ascontiguousarray(words).view(ml_dtypes.float8_e4m3fn).astype(np.float64) * np.repeat(np.exp2(scales.astype(np.float64) - 127.0), 8, axis=1)[..., None]
    return vals.transpose(0, 1, 3, 2).reshape(g * 512, n)


K, T, S, N, H, U = 512, 2048, 512, 512, 512, 1024


def setup_inputs():
    n = np.random.standard_normal
    s = mx_kscale(K)[:, None]
    u = mx_kscale(H)
    packed_xT = pack_weight(n((K, T)) * s)
    return {
        "x_words": packed_xT[0],
        "x_scales": packed_xT[1],
        "w1": (n((K, H)) / np.sqrt(K) / s).astype(np.float32),
        "gn": (np.random.uniform(0.5, 1.5, (H, 1)) * u[:, None]).astype(np.float32),
        "w2": (n((H, N)) / np.sqrt(H) / u[:, None]).astype(np.float32),
        "mem": n((N, U)).astype(np.float32),
        "offs": striped8(np.random.randint(0, T, (8, S))),
        "n1": striped8(np.stack([np.random.permutation(S) for _ in range(8)])),
        "n2": striped8(np.stack([np.random.permutation(S) for _ in range(8)])),
        "n3": striped8(np.stack([np.random.permutation(S) for _ in range(8)])),
        "n4": striped8(np.stack([np.random.permutation(U)[:S] for _ in range(8)])),
    }


def reference(x_words, x_scales, w1, gn, w2, mem, offs, n1, n2, n3, n4):
    xq = unpack_weight(x_words, x_scales)[np.arange(K)[:, None], runs(offs, K)]
    y = mxq(f64(w1), 0, "e4m3").T @ xq
    z = f64(gn) * (0.75 * (y * (y[np.arange(H)[:, None], runs(n1, H)]) + (y[np.arange(H)[:, None], runs(n2, H)]) * (y[np.arange(H)[:, None], runs(n3, H)])))
    h = mxq(f64(w2), 0, "e4m3").T @ mxq(z, 0, "e4m3")
    out = f64(mem).copy()
    out[np.arange(N)[:, None], runs(n4, N)] = h
    return out

@@ -1,0 +1,212 @@
+from contextlib import ExitStack
+
+import concourse.mybir as mybir
+from concourse.masks import make_identity
+
+K, T, S, N, H, U = 512, 2048, 512, 512, 512, 1024
+FLOPS = 2 * K * H * S + 2 * H * N * S
+
+F32 = mybir.dt.float32
+BF16 = mybir.dt.bfloat16
+I32 = mybir.dt.int32
+U32 = mybir.dt.uint32
+U16 = mybir.dt.uint16
+U8 = mybir.dt.uint8
+FP8X4 = mybir.dt.float8_e4m3fn_x4
+MULT = mybir.AluOpType.mult
+COPY = mybir.ActivationFunctionType.Copy
+
+P = 128
+PACK = 4
+HALF = S // 2
+LCOLS = HALF // 16
+
+
+def tile_picked_hashdotpage_none_p_kernel(
+    tc, x_words, x_scales, w1, gn, w2, mem, offs, n1, n2, n3, n4, out
+):
+    nc = tc.nc
+    with ExitStack() as ctx:
+        lists = ctx.enter_context(tc.tile_pool(name="lists", bufs=1))
+        sb = ctx.enter_context(tc.tile_pool(name="sb", bufs=1))
+        ps = ctx.enter_context(tc.psum_pool(name="ps", bufs=1))
+
+        def sbuf(shape, dtype, name, tag=None):
+            return sb.tile(shape, dtype, name=name, tag=tag or name, align_bytes=64)
+
+        def load_list(source, name):
+            tile = lists.tile([P, S // 16], U16, name=name)
+            nc.sync.dma_start(tile[:], source)
+            return tile
+
+        def half_of(tile, h):
+            return tile[:, h * LCOLS : (h + 1) * LCOLS]
+
+        offs_sb = load_list(offs, "offs_sb")
+        scale_table = sbuf([P, T], U8, "scale_table")
+        nc.sync.dma_start(
+            scale_table[:].bitcast(I32),
+            x_scales[0].bitcast(I32).unsqueeze(1).broadcast_to([16, 8, T // 4]),
+        )
+        w1_raw = sbuf([P, PACK, H], F32, "w1_raw", tag="w_raw")
+        nc.sync.dma_start(w1_raw[:], w1.rearrange("(p j) c -> p j c", j=PACK))
+        gain = sbuf([P, PACK], F32, "gain")
+        nc.sync.dma_start(gain[:], gn.rearrange("(p t) o -> p (t o)", t=PACK))
+        n2_sb = load_list(n2, "n2_sb")
+        n1_sb = load_list(n1, "n1_sb")
+        word_table = sbuf([P, T], U32, "word_table", tag="page0")
+        nc.sync.dma_start(
+            word_table[:].bitcast(I32),
+            x_words[0].rearrange("p n r -> p (n r)").bitcast(I32),
+        )
+        n3_sb = load_list(n3, "n3_sb")
+        n4_sb = load_list(n4, "n4_sb")
+
+        x_plane = sbuf([P, S], U8, "x_plane")
+        nc.gpsimd.memset(x_plane[:], 0)
+        ident = sbuf([P, P], F32, "ident")
+        make_identity(nc, ident[:])
+
+        picked_scales = sbuf([P, S], U8, "picked_scales")
+        nc.vector.tensor_copy(picked_scales[:], scale_table[:].indirect(offs_sb[:]))
+        for r in range(4):
+            nc.scalar.dma_start(
+                x_plane[r:P:32, :].bitcast(I32), picked_scales[8 * r : P : 32, :].bitcast(I32)
+            )
+
+        def deal(copy, raw, name, tag):
+            dealt = sbuf([P, PACK * H], BF16, name, tag=tag)
+            copy(
+                dealt[:].rearrange("p (t m j) -> p m t j", t=PACK, j=PACK),
+                raw[:].rearrange("p j (m t) -> p m t j", t=PACK),
+            )
+            return dealt
+
+        def quantize(source, width, name, tag):
+            codes = sbuf([P, width], U32, name + "_codes", tag=tag)
+            plane = sbuf([P, width], U8, name + "_plane")
+            nc.vector.quantize_mx(out=codes[:].bitcast(FP8X4), scales=plane[:], in_=source)
+            return codes, plane
+
+        w1_dealt = deal(nc.vector.tensor_copy, w1_raw, "w1_dealt", "page1")
+        w1_codes, w1_plane = quantize(w1_dealt[:], H, "w1", "page2")
+
+        w2_raw = sbuf([P, PACK, N], F32, "w2_raw", tag="w_raw")
+        nc.sync.dma_start(w2_raw[:], w2.rearrange("(p j) c -> p j c", j=PACK))
+
+        picked_words = sbuf([P, S], U32, "picked_words", tag="page3")
+        nc.vector.tensor_copy(picked_words[:], word_table[:].indirect(offs_sb[:]))
+
+        y = []
+        gy = []
+        for t in range(PACK):
+            acc = ps.tile([P, S], F32, name=f"y_acc{t}", tag=f"mm{t}")
+            cols = slice(t * P, (t + 1) * P)
+            nc.tensor.matmul_mx(
+                out=acc[:],
+                lhsT=w1_codes[:, cols].bitcast(FP8X4),
+                lhsT_scale=w1_plane[:, cols],
+                rhs=picked_words[:].bitcast(FP8X4),
+                rhs_scale=x_plane[:],
+                start=True,
+                stop=True,
+            )
+            gy.append(sbuf([P, S], F32, f"gy{t}"))
+            nc.scalar.activation(gy[t][:], acc[:], COPY, scale=gain[:, t : t + 1])
+            y.append(sbuf([P, S], F32, f"y{t}"))
+            nc.scalar.copy(y[t][:], acc[:])
+
+        mem_rows = mem.rearrange("(p t) w -> p t w", t=PACK)
+        out_rows = out.rearrange("(p t) w -> p t w", t=PACK)
+        pages = []
+        for t in range(PACK):
+            pages.append(sbuf([P, U], F32, f"page{t}"))
+            nc.sync.dma_start(pages[t][:], mem_rows[:, t, :])
+
+        w2_dealt = deal(nc.scalar.copy, w2_raw, "w2_dealt", "w2_dealt")
+        w2_codes, w2_plane = quantize(w2_dealt[:], N, "w2", "w2_codes")
+
+        def products(h, t, sums, tag):
+            left = sbuf([P, HALF], F32, f"left{h}{t}", tag=tag)
+            nc.vector.tensor_copy(left[:], gy[t][:].indirect(half_of(n2_sb, h)))
+            first = sbuf([P, HALF], F32, f"first{h}{t}")
+            nc.vector.tensor_tensor(
+                first[:], y[t][:].indirect(half_of(n1_sb, h)), gy[t][:, h * HALF : (h + 1) * HALF], MULT
+            )
+            second = sbuf([P, HALF], F32, f"second{h}{t}")
+            nc.vector.tensor_tensor(second[:], y[t][:].indirect(half_of(n3_sb, h)), left[:], MULT)
+            for term, opens in ((first, True), (second, False)):
+                for b in range(2):
+                    nc.tensor.matmul(
+                        sums[b][:, t, :],
+                        lhsT=term[:, b * P : (b + 1) * P],
+                        rhs=ident[:],
+                        start=opens,
+                        stop=not opens,
+                        is_transpose=True,
+                    )
+
+        def quantize_z(h, sums):
+            back = ps.tile([P, 2, HALF], F32, name=f"back{h}", tag=f"back{h}")
+            for b in range(2):
+                rounded = sbuf([P, 2, P, 2], BF16, f"rounded{h}{b}")
+                nc.scalar.activation(
+                    rounded[:], sums[b][:].rearrange("s (u e) p -> s u p e", e=2), COPY, scale=0.75
+                )
+                pairs = rounded[:].rearrange("s u p e -> s (u p e)").bitcast(F32)
+                for u in range(2):
+                    nc.tensor.transpose(
+                        back[:, u, b * P : (b + 1) * P], pairs[:, u * P : (u + 1) * P], ident[:]
+                    )
+            z = sbuf([P, PACK * HALF], BF16, f"z{h}")
+            nc.scalar.copy(
+                z[:].bitcast(F32).rearrange("p (s u) -> p s u", u=2), back[:].rearrange("p u s -> p s u")
+            )
+            return quantize(z[:], HALF, f"z{h}", f"z{h}_codes")
+
+        def second_product(h, pair, z_codes, z_plane):
+            acc = ps.tile([P, 2, HALF], F32, name=f"h_acc{h}{pair}", tag=f"mm{2 * h + pair}")
+            for i in range(2):
+                cols = slice((2 * pair + i) * P, (2 * pair + i + 1) * P)
+                nc.tensor.matmul_mx(
+                    out=acc[:, i, :],
+                    lhsT=w2_codes[:, cols].bitcast(FP8X4),
+                    lhsT_scale=w2_plane[:, cols],
+                    rhs=z_codes[:].bitcast(FP8X4),
+                    rhs_scale=z_plane[:],
+                    start=True,
+                    stop=True,
+                )
+            return acc
+
+        def stage(h, pair, acc, tag):
+            staged = sbuf([P, 2, HALF], F32, f"staged{h}{pair}", tag=tag)
+            nc.scalar.copy(staged[:], acc[:])
+            return staged
+
+        def scatter(h, pair, staged):
+            for i in range(2):
+                nc.vector.tensor_copy(pages[2 * pair + i][:].indirect(half_of(n4_sb, h)), staged[:, i, :])
+
+        def open_sums(h):
+            return [ps.tile([P, PACK, P], F32, name=f"sums{h}{b}", tag=f"sums{b}") for b in range(2)]
+
+        sums = open_sums(0)
+        for t in range(PACK):
+            products(0, t, sums, f"left0{t}")
+        z_codes, z_plane = quantize_z(0, sums)
+        acc0 = [second_product(0, pair, z_codes, z_plane) for pair in range(2)]
+        staged00 = stage(0, 0, acc0[0], "staged00")
+
+        sums = open_sums(1)
+        for t in range(PACK):
+            products(1, t, sums, "z0" if t == 2 else f"left1{t}")
+        z_codes, z_plane = quantize_z(1, sums)
+        staged01 = stage(0, 1, acc0[1], "rounded11")
+        scatter(0, 0, staged00)
+        scatter(0, 1, staged01)
+        for pair in range(2):
+            acc = second_product(1, pair, z_codes, z_plane)
+            scatter(1, pair, stage(1, pair, acc, f"staged1{pair}"))
+            for i in range(2):
+                nc.sync.dma_start(out_rows[:, 2 * pair + i, :], pages[2 * pair + i][:])

@@ -42,79 +42,89 @@ def tile_picked_hashdotpage_none_p_kernel(
         def half_of(tile, h):
             return tile[:, h * LCOLS : (h + 1) * LCOLS]
 
-        offs_sb = load_list(offs, "offs_sb")
         scale_table = sbuf([P, T], U8, "scale_table")
+        x_plane = sbuf([P, S], U8, "x_plane")
+        nc.gpsimd.memset(x_plane[:].bitcast(I32), 0)
+        ident = sbuf([P, P], F32, "ident")
+        make_identity(nc, ident[:])
+
+        offs_sb = load_list(offs, "offs_sb")
         nc.sync.dma_start(
             scale_table[:].bitcast(I32),
             x_scales[0].bitcast(I32).unsqueeze(1).broadcast_to([16, 8, T // 4]),
         )
+        gain = sbuf([P, PACK], F32, "gain")
+        nc.gpsimd.dma_start(gain[:], gn.rearrange("(p t) o -> p (t o)", t=PACK))
+        n2_sb = load_list(n2, "n2_sb")
         w1_raw = sbuf([P, PACK, H], F32, "w1_raw", tag="w_raw")
         nc.sync.dma_start(w1_raw[:], w1.rearrange("(p j) c -> p j c", j=PACK))
-        gain = sbuf([P, PACK], F32, "gain")
-        nc.sync.dma_start(gain[:], gn.rearrange("(p t) o -> p (t o)", t=PACK))
-        n2_sb = load_list(n2, "n2_sb")
-        n1_sb = load_list(n1, "n1_sb")
         word_table = sbuf([P, T], U32, "word_table", tag="page0")
         nc.sync.dma_start(
             word_table[:].bitcast(I32),
             x_words[0].rearrange("p n r -> p (n r)").bitcast(I32),
         )
+        n1_sb = load_list(n1, "n1_sb")
         n3_sb = load_list(n3, "n3_sb")
         n4_sb = load_list(n4, "n4_sb")
-
-        x_plane = sbuf([P, S], U8, "x_plane")
-        nc.gpsimd.memset(x_plane[:], 0)
-        ident = sbuf([P, P], F32, "ident")
-        make_identity(nc, ident[:])
 
         picked_scales = sbuf([P, S], U8, "picked_scales")
         nc.vector.tensor_copy(picked_scales[:], scale_table[:].indirect(offs_sb[:]))
         for r in range(4):
-            nc.scalar.dma_start(
+            nc.sync.dma_start(
                 x_plane[r:P:32, :].bitcast(I32), picked_scales[8 * r : P : 32, :].bitcast(I32)
             )
 
-        def deal(copy, raw, name, tag):
-            dealt = sbuf([P, PACK * H], BF16, name, tag=tag)
+        def deal(copy, raw, dealt, tiles):
             copy(
-                dealt[:].rearrange("p (t m j) -> p m t j", t=PACK, j=PACK),
-                raw[:].rearrange("p j (m t) -> p m t j", t=PACK),
+                dealt[:].rearrange("p (t m j) -> p m t j", t=PACK, j=PACK)[:, :, tiles, :],
+                raw[:].rearrange("p j (m t) -> p m t j", t=PACK)[:, :, tiles, :],
             )
-            return dealt
 
-        def quantize(source, width, name, tag):
-            codes = sbuf([P, width], U32, name + "_codes", tag=tag)
-            plane = sbuf([P, width], U8, name + "_plane")
-            nc.vector.quantize_mx(out=codes[:].bitcast(FP8X4), scales=plane[:], in_=source)
-            return codes, plane
+        def mx_tiles(width, name, tag):
+            return sbuf([P, width], U32, name + "_codes", tag=tag), sbuf([P, width], U8, name + "_plane")
 
-        w1_dealt = deal(nc.vector.tensor_copy, w1_raw, "w1_dealt", "page1")
-        w1_codes, w1_plane = quantize(w1_dealt[:], H, "w1", "page2")
+        def quantize(source, codes, plane):
+            nc.vector.quantize_mx(out=codes.bitcast(FP8X4), scales=plane, in_=source)
+
+        w1_dealt = sbuf([P, PACK * H], BF16, "w1_dealt", tag="page1")
+        w1_codes, w1_plane = mx_tiles(H, "w1", "page2")
+        for pair, copy in enumerate((nc.vector.tensor_copy, nc.scalar.copy)):
+            deal(copy, w1_raw, w1_dealt, slice(2 * pair, 2 * pair + 2))
+        for pair in range(2):
+            cols = slice(pair * 2 * P, (pair + 1) * 2 * P)
+            quantize(w1_dealt[:, PACK * cols.start : PACK * cols.stop], w1_codes[:, cols], w1_plane[:, cols])
 
         w2_raw = sbuf([P, PACK, N], F32, "w2_raw", tag="w_raw")
         nc.sync.dma_start(w2_raw[:], w2.rearrange("(p j) c -> p j c", j=PACK))
 
         picked_words = sbuf([P, S], U32, "picked_words", tag="page3")
-        nc.vector.tensor_copy(picked_words[:], word_table[:].indirect(offs_sb[:]))
+        for h in range(2):
+            nc.vector.tensor_copy(
+                picked_words[:, h * HALF : (h + 1) * HALF], word_table[:].indirect(half_of(offs_sb, h))
+            )
 
-        y = []
-        gy = []
-        for t in range(PACK):
-            acc = ps.tile([P, S], F32, name=f"y_acc{t}", tag=f"mm{t}")
+        y = [sbuf([P, S], F32, f"y{t}") for t in range(PACK)]
+        gy = [sbuf([P, S], F32, f"gy{t}") for t in range(PACK)]
+
+        def first_product(t, places, bank, copy):
+            acc = ps.tile([P, places.stop - places.start], F32, name=f"y_acc_{bank}", tag=bank)
             cols = slice(t * P, (t + 1) * P)
             nc.tensor.matmul_mx(
                 out=acc[:],
                 lhsT=w1_codes[:, cols].bitcast(FP8X4),
                 lhsT_scale=w1_plane[:, cols],
-                rhs=picked_words[:].bitcast(FP8X4),
-                rhs_scale=x_plane[:],
+                rhs=picked_words[:, places].bitcast(FP8X4),
+                rhs_scale=x_plane[:, places],
                 start=True,
                 stop=True,
             )
-            gy.append(sbuf([P, S], F32, f"gy{t}"))
-            nc.scalar.activation(gy[t][:], acc[:], COPY, scale=gain[:, t : t + 1])
-            y.append(sbuf([P, S], F32, f"y{t}"))
-            nc.scalar.copy(y[t][:], acc[:])
+            nc.scalar.activation(gy[t][:, places], acc[:], COPY, scale=gain[:, t : t + 1])
+            copy(y[t][:, places], acc[:])
+
+        first_product(0, slice(0, HALF), "back1", nc.vector.tensor_copy)
+        first_product(0, slice(HALF, S), "mm0", nc.scalar.copy)
+        for t in range(1, PACK):
+            first_product(t, slice(0, S), f"mm{t}", nc.scalar.copy)
 
         mem_rows = mem.rearrange("(p t) w -> p t w", t=PACK)
         out_rows = out.rearrange("(p t) w -> p t w", t=PACK)
@@ -123,8 +133,10 @@ def tile_picked_hashdotpage_none_p_kernel(
             pages.append(sbuf([P, U], F32, f"page{t}"))
             nc.sync.dma_start(pages[t][:], mem_rows[:, t, :])
 
-        w2_dealt = deal(nc.scalar.copy, w2_raw, "w2_dealt", "w2_dealt")
-        w2_codes, w2_plane = quantize(w2_dealt[:], N, "w2", "w2_codes")
+        w2_dealt = sbuf([P, PACK * N], BF16, "w2_dealt")
+        deal(nc.scalar.copy, w2_raw, w2_dealt, slice(0, PACK))
+        w2_codes, w2_plane = mx_tiles(N, "w2", "w2_codes")
+        quantize(w2_dealt[:], w2_codes[:], w2_plane[:])
 
         def products(h, t, sums, tag):
             left = sbuf([P, HALF], F32, f"left{h}{t}", tag=tag)
@@ -162,7 +174,9 @@ def tile_picked_hashdotpage_none_p_kernel(
             nc.scalar.copy(
                 z[:].bitcast(F32).rearrange("p (s u) -> p s u", u=2), back[:].rearrange("p u s -> p s u")
             )
-            return quantize(z[:], HALF, f"z{h}", f"z{h}_codes")
+            codes, plane = mx_tiles(HALF, f"z{h}", f"z{h}_codes")
+            quantize(z[:], codes[:], plane[:])
+            return codes, plane
 
         def second_product(h, pair, z_codes, z_plane):
             acc = ps.tile([P, 2, HALF], F32, name=f"h_acc{h}{pair}", tag=f"mm{2 * h + pair}")
@@ -179,14 +193,13 @@ def tile_picked_hashdotpage_none_p_kernel(
                 )
             return acc
 
-        def stage(h, pair, acc, tag):
-            staged = sbuf([P, 2, HALF], F32, f"staged{h}{pair}", tag=tag)
-            nc.scalar.copy(staged[:], acc[:])
+        def stage(h, t, acc, tag):
+            staged = sbuf([P, HALF], F32, f"staged{h}{t}", tag=tag)
+            nc.scalar.copy(staged[:], acc[t // 2][:, t % 2, :])
             return staged
 
-        def scatter(h, pair, staged):
-            for i in range(2):
-                nc.vector.tensor_copy(pages[2 * pair + i][:].indirect(half_of(n4_sb, h)), staged[:, i, :])
+        def scatter(h, t, staged):
+            nc.vector.tensor_copy(pages[t][:].indirect(half_of(n4_sb, h)), staged[:])
 
         def open_sums(h):
             return [ps.tile([P, PACK, P], F32, name=f"sums{h}{b}", tag=f"sums{b}") for b in range(2)]
@@ -196,17 +209,16 @@ def tile_picked_hashdotpage_none_p_kernel(
             products(0, t, sums, f"left0{t}")
         z_codes, z_plane = quantize_z(0, sums)
         acc0 = [second_product(0, pair, z_codes, z_plane) for pair in range(2)]
-        staged00 = stage(0, 0, acc0[0], "staged00")
+        staged0 = [stage(0, t, acc0, f"staged0{t}") for t in range(PACK - 1)]
 
         sums = open_sums(1)
         for t in range(PACK):
-            products(1, t, sums, "z0" if t == 2 else f"left1{t}")
+            products(1, t, sums, "z0" if t == PACK - 1 else f"left1{t}")
         z_codes, z_plane = quantize_z(1, sums)
-        staged01 = stage(0, 1, acc0[1], "rounded11")
-        scatter(0, 0, staged00)
-        scatter(0, 1, staged01)
-        for pair in range(2):
-            acc = second_product(1, pair, z_codes, z_plane)
-            scatter(1, pair, stage(1, pair, acc, f"staged1{pair}"))
-            for i in range(2):
-                nc.sync.dma_start(out_rows[:, 2 * pair + i, :], pages[2 * pair + i][:])
+        staged0.append(stage(0, PACK - 1, acc0, "rounded11"))
+        for t in range(PACK):
+            scatter(0, t, staged0[t])
+        acc1 = [second_product(1, pair, z_codes, z_plane) for pair in range(2)]
+        for t in range(PACK):
+            scatter(1, t, stage(1, t, acc1, f"staged1{t}"))
+            nc.sync.dma_start(out_rows[:, t, :], pages[t][:])

@@ -106,7 +106,7 @@ def tile_picked_hashdotpage_none_p_kernel(
         y = [sbuf([P, S], F32, f"y{t}") for t in range(PACK)]
         gy = [sbuf([P, S], F32, f"gy{t}") for t in range(PACK)]
 
-        def first_product(t, places, bank, copy):
+        def first_product(t, places, bank, times_gain, copy):
             acc = ps.tile([P, places.stop - places.start], F32, name=f"y_acc_{bank}", tag=bank)
             cols = slice(t * P, (t + 1) * P)
             nc.tensor.matmul_mx(
@@ -118,13 +118,14 @@ def tile_picked_hashdotpage_none_p_kernel(
                 start=True,
                 stop=True,
             )
-            nc.scalar.activation(gy[t][:, places], acc[:], COPY, scale=gain[:, t : t + 1])
+            times_gain(gy[t][:, places], acc[:], gain[:, t : t + 1])
             copy(y[t][:, places], acc[:])
 
-        first_product(0, slice(0, HALF), "back1", nc.vector.tensor_copy)
-        first_product(0, slice(HALF, S), "mm0", nc.scalar.copy)
+        first_product(0, slice(0, HALF), "back1", nc.scalar.mul, nc.vector.tensor_copy)
+        first_product(0, slice(HALF, HALF + P), "mm0", nc.scalar.mul, nc.scalar.copy)
+        first_product(0, slice(HALF + P, S), "back0", nc.vector.tensor_scalar_mul, nc.scalar.copy)
         for t in range(1, PACK):
-            first_product(t, slice(0, S), f"mm{t}", nc.scalar.copy)
+            first_product(t, slice(0, S), f"mm{t}", nc.scalar.mul, nc.scalar.copy)
 
         mem_rows = mem.rearrange("(p t) w -> p t w", t=PACK)
         out_rows = out.rearrange("(p t) w -> p t w", t=PACK)

from contextlib import ExitStack

import concourse.mybir as mybir
from concourse.masks import make_identity

K, T, S, N, H, U = 512, 2048, 512, 512, 512, 1024
FLOPS = 2 * K * H * S + 2 * H * N * S

F32 = mybir.dt.float32
BF16 = mybir.dt.bfloat16
I32 = mybir.dt.int32
U32 = mybir.dt.uint32
U16 = mybir.dt.uint16
U8 = mybir.dt.uint8
FP8X4 = mybir.dt.float8_e4m3fn_x4
MULT = mybir.AluOpType.mult
COPY = mybir.ActivationFunctionType.Copy

P = 128
PACK = 4
HALF = S // 2
LCOLS = HALF // 16


def tile_picked_hashdotpage_none_p_kernel(
    tc, x_words, x_scales, w1, gn, w2, mem, offs, n1, n2, n3, n4, out
):
    nc = tc.nc
    with ExitStack() as ctx:
        lists = ctx.enter_context(tc.tile_pool(name="lists", bufs=1))
        sb = ctx.enter_context(tc.tile_pool(name="sb", bufs=1))
        ps = ctx.enter_context(tc.psum_pool(name="ps", bufs=1))

        def sbuf(shape, dtype, name, tag=None):
            return sb.tile(shape, dtype, name=name, tag=tag or name, align_bytes=64)

        def load_list(source, name):
            tile = lists.tile([P, S // 16], U16, name=name)
            nc.sync.dma_start(tile[:], source)
            return tile

        def half_of(tile, h):
            return tile[:, h * LCOLS : (h + 1) * LCOLS]

        scale_table = sbuf([P, T], U8, "scale_table")
        x_plane = sbuf([P, S], U8, "x_plane")
        nc.gpsimd.memset(x_plane[:].bitcast(I32), 0)
        ident = sbuf([P, P], F32, "ident")
        make_identity(nc, ident[:])

        offs_sb = load_list(offs, "offs_sb")
        nc.sync.dma_start(
            scale_table[:].bitcast(I32),
            x_scales[0].bitcast(I32).unsqueeze(1).broadcast_to([16, 8, T // 4]),
        )
        gain = sbuf([P, PACK], F32, "gain")
        nc.gpsimd.dma_start(gain[:], gn.rearrange("(p t) o -> p (t o)", t=PACK))
        n2_sb = load_list(n2, "n2_sb")
        w1_raw = sbuf([P, PACK, H], F32, "w1_raw", tag="w_raw")
        nc.sync.dma_start(w1_raw[:], w1.rearrange("(p j) c -> p j c", j=PACK))
        word_table = sbuf([P, T], U32, "word_table", tag="page0")
        nc.sync.dma_start(
            word_table[:].bitcast(I32),
            x_words[0].rearrange("p n r -> p (n r)").bitcast(I32),
        )
        n1_sb = load_list(n1, "n1_sb")
        n3_sb = load_list(n3, "n3_sb")
        n4_sb = load_list(n4, "n4_sb")

        picked_scales = sbuf([P, S], U8, "picked_scales")
        nc.vector.tensor_copy(picked_scales[:], scale_table[:].indirect(offs_sb[:]))
        for r in range(4):
            nc.sync.dma_start(
                x_plane[r:P:32, :].bitcast(I32), picked_scales[8 * r : P : 32, :].bitcast(I32)
            )

        def deal(copy, raw, dealt, tiles):
            copy(
                dealt[:].rearrange("p (t m j) -> p m t j", t=PACK, j=PACK)[:, :, tiles, :],
                raw[:].rearrange("p j (m t) -> p m t j", t=PACK)[:, :, tiles, :],
            )

        def mx_tiles(width, name, tag):
            return sbuf([P, width], U32, name + "_codes", tag=tag), sbuf([P, width], U8, name + "_plane")

        def quantize(source, codes, plane):
            nc.vector.quantize_mx(out=codes.bitcast(FP8X4), scales=plane, in_=source)

        w1_dealt = sbuf([P, PACK * H], BF16, "w1_dealt", tag="page1")
        w1_codes, w1_plane = mx_tiles(H, "w1", "page2")
        for pair, copy in enumerate((nc.vector.tensor_copy, nc.scalar.copy)):
            deal(copy, w1_raw, w1_dealt, slice(2 * pair, 2 * pair + 2))
        for pair in range(2):
            cols = slice(pair * 2 * P, (pair + 1) * 2 * P)
            quantize(w1_dealt[:, PACK * cols.start : PACK * cols.stop], w1_codes[:, cols], w1_plane[:, cols])

        w2_raw = sbuf([P, PACK, N], F32, "w2_raw", tag="w_raw")
        nc.sync.dma_start(w2_raw[:], w2.rearrange("(p j) c -> p j c", j=PACK))

        picked_words = sbuf([P, S], U32, "picked_words", tag="page3")
        for h in range(2):
            nc.vector.tensor_copy(
                picked_words[:, h * HALF : (h + 1) * HALF], word_table[:].indirect(half_of(offs_sb, h))
            )

        y = [sbuf([P, S], F32, f"y{t}") for t in range(PACK)]
        gy = [sbuf([P, S], F32, f"gy{t}") for t in range(PACK)]

        def first_product(t, places, bank, times_gain, copy):
            acc = ps.tile([P, places.stop - places.start], F32, name=f"y_acc_{bank}", tag=bank)
            cols = slice(t * P, (t + 1) * P)
            nc.tensor.matmul_mx(
                out=acc[:],
                lhsT=w1_codes[:, cols].bitcast(FP8X4),
                lhsT_scale=w1_plane[:, cols],
                rhs=picked_words[:, places].bitcast(FP8X4),
                rhs_scale=x_plane[:, places],
                start=True,
                stop=True,
            )
            times_gain(gy[t][:, places], acc[:], gain[:, t : t + 1])
            copy(y[t][:, places], acc[:])

        first_product(0, slice(0, HALF), "back1", nc.scalar.mul, nc.vector.tensor_copy)
        first_product(0, slice(HALF, HALF + P), "mm0", nc.scalar.mul, nc.scalar.copy)
        first_product(0, slice(HALF + P, S), "back0", nc.vector.tensor_scalar_mul, nc.scalar.copy)
        for t in range(1, PACK):
            first_product(t, slice(0, S), f"mm{t}", nc.scalar.mul, nc.scalar.copy)

        mem_rows = mem.rearrange("(p t) w -> p t w", t=PACK)
        out_rows = out.rearrange("(p t) w -> p t w", t=PACK)
        pages = []
        for t in range(PACK):
            pages.append(sbuf([P, U], F32, f"page{t}"))
            nc.sync.dma_start(pages[t][:], mem_rows[:, t, :])

        w2_dealt = sbuf([P, PACK * N], BF16, "w2_dealt")
        deal(nc.scalar.copy, w2_raw, w2_dealt, slice(0, PACK))
        w2_codes, w2_plane = mx_tiles(N, "w2", "w2_codes")
        quantize(w2_dealt[:], w2_codes[:], w2_plane[:])

        def products(h, t, sums, tag):
            left = sbuf([P, HALF], F32, f"left{h}{t}", tag=tag)
            nc.vector.tensor_copy(left[:], gy[t][:].indirect(half_of(n2_sb, h)))
            first = sbuf([P, HALF], F32, f"first{h}{t}")
            nc.vector.tensor_tensor(
                first[:], y[t][:].indirect(half_of(n1_sb, h)), gy[t][:, h * HALF : (h + 1) * HALF], MULT
            )
            second = sbuf([P, HALF], F32, f"second{h}{t}")
            nc.vector.tensor_tensor(second[:], y[t][:].indirect(half_of(n3_sb, h)), left[:], MULT)
            for term, opens in ((first, True), (second, False)):
                for b in range(2):
                    nc.tensor.matmul(
                        sums[b][:, t, :],
                        lhsT=term[:, b * P : (b + 1) * P],
                        rhs=ident[:],
                        start=opens,
                        stop=not opens,
                        is_transpose=True,
                    )

        def quantize_z(h, sums):
            back = ps.tile([P, 2, HALF], F32, name=f"back{h}", tag=f"back{h}")
            for b in range(2):
                rounded = sbuf([P, 2, P, 2], BF16, f"rounded{h}{b}")
                nc.scalar.activation(
                    rounded[:], sums[b][:].rearrange("s (u e) p -> s u p e", e=2), COPY, scale=0.75
                )
                pairs = rounded[:].rearrange("s u p e -> s (u p e)").bitcast(F32)
                for u in range(2):
                    nc.tensor.transpose(
                        back[:, u, b * P : (b + 1) * P], pairs[:, u * P : (u + 1) * P], ident[:]
                    )
            z = sbuf([P, PACK * HALF], BF16, f"z{h}")
            nc.scalar.copy(
                z[:].bitcast(F32).rearrange("p (s u) -> p s u", u=2), back[:].rearrange("p u s -> p s u")
            )
            codes, plane = mx_tiles(HALF, f"z{h}", f"z{h}_codes")
            quantize(z[:], codes[:], plane[:])
            return codes, plane

        def second_product(h, pair, z_codes, z_plane):
            acc = ps.tile([P, 2, HALF], F32, name=f"h_acc{h}{pair}", tag=f"mm{2 * h + pair}")
            for i in range(2):
                cols = slice((2 * pair + i) * P, (2 * pair + i + 1) * P)
                nc.tensor.matmul_mx(
                    out=acc[:, i, :],
                    lhsT=w2_codes[:, cols].bitcast(FP8X4),
                    lhsT_scale=w2_plane[:, cols],
                    rhs=z_codes[:].bitcast(FP8X4),
                    rhs_scale=z_plane[:],
                    start=True,
                    stop=True,
                )
            return acc

        def stage(h, t, acc, tag):
            staged = sbuf([P, HALF], F32, f"staged{h}{t}", tag=tag)
            nc.scalar.copy(staged[:], acc[t // 2][:, t % 2, :])
            return staged

        def scatter(h, t, staged):
            nc.vector.tensor_copy(pages[t][:].indirect(half_of(n4_sb, h)), staged[:])

        def open_sums(h):
            return [ps.tile([P, PACK, P], F32, name=f"sums{h}{b}", tag=f"sums{b}") for b in range(2)]

        sums = open_sums(0)
        for t in range(PACK):
            products(0, t, sums, f"left0{t}")
        z_codes, z_plane = quantize_z(0, sums)
        acc0 = [second_product(0, pair, z_codes, z_plane) for pair in range(2)]
        staged0 = [stage(0, t, acc0, f"staged0{t}") for t in range(PACK - 1)]

        sums = open_sums(1)
        for t in range(PACK):
            products(1, t, sums, "z0" if t == PACK - 1 else f"left1{t}")
        z_codes, z_plane = quantize_z(1, sums)
        staged0.append(stage(0, PACK - 1, acc0, "rounded11"))
        for t in range(PACK):
            scatter(0, t, staged0[t])
        acc1 = [second_product(1, pair, z_codes, z_plane) for pair in range(2)]
        for t in range(PACK):
            scatter(1, t, stage(1, t, acc1, f"staged1{t}"))
            nc.sync.dma_start(out_rows[:, t, :], pages[t][:])
